import numpy as np
import ml_dtypes


def mxq(x, axis, fmt="e4m3"):
    dtype, down = {"e4m3": (ml_dtypes.float8_e4m3fn, 7), "e5m2": (ml_dtypes.float8_e5m2, 14)}[fmt]
    v = np.moveaxis(np.asarray(x, np.float32).astype(ml_dtypes.bfloat16).astype(np.float64), axis, -1)
    blocks = v.reshape(v.shape[:-1] + (-1, 32))
    amax = np.abs(blocks).max(-1, keepdims=True)
    byte = np.maximum(np.where(amax > 0, np.frexp(amax)[1] - 1 + 127, 0) - down, 1)
    scale = np.exp2(byte - 127.0)
    codes = (blocks / scale).astype(np.float32).astype(dtype).astype(np.float64)
    return np.moveaxis((codes * scale).reshape(v.shape), -1, axis)


WIDE = False


def mx_kscale(k):
    if not WIDE:
        return np.ones(k)
    levels = np.array([30, -30])
    if k % 512:
        return np.exp2(np.random.permutation(np.resize(levels, k // 32))).repeat(32)
    a = np.empty((k // 512, 16))
    for p in range(k // 512):
        a[p, :8] = np.random.permutation(np.resize(levels, 8))
        for g in range(8):
            far = levels[np.abs(levels - a[p, g]) >= 10]
            a[p, g + 8] = far[np.random.randint(len(far))]
    return np.exp2(a.ravel()).repeat(32)


BF16 = ml_dtypes.bfloat16


def bf(x):
    return np.asarray(x, np.float32).astype(BF16)


def f64(x):
    return np.asarray(x).astype(np.float64)


M, L, K, H, B, J = 2048, 1024, 1024, 512, 256, 4


def setup_inputs():
    s = mx_kscale(K)
    t = mx_kscale(H)
    tails = np.random.standard_normal((M, H)) * np.exp(np.random.standard_normal((M, H)) - 1.0)
    return {
        "low": bf(np.random.standard_normal((K, M)) * s[:, None]),
        "basis_low": bf(np.random.standard_normal((K, L)) / np.sqrt(K) / s[:, None]),
        "high": bf(tails * t),
        "basis_high": bf(np.random.standard_normal((L, H)) / np.sqrt(H) / t),
        "weights": bf(0.25 + 0.5 * np.random.random_sample((B, J))),
    }


def reference(low, basis_low, high, basis_high, weights):
    lq = mxq(f64(low), 0, "e4m3")
    pq = mxq(f64(basis_low), 0, "e4m3")
    hq = mxq(f64(high), 1, "e5m2")
    rq = mxq(f64(basis_high), 1, "e4m3")
    z = (lq.T @ pq) + (hq @ rq.T)
    u = z / np.sqrt(1.0 + z * z)
    return (u.reshape(M, B, J) * f64(weights)).sum(axis=2)

@@ -1,0 +1,333 @@
+from contextlib import ExitStack
+
+import concourse.mybir as mybir
+from concourse.masks import make_identity
+
+M, L, K, H, B, J = 2048, 1024, 1024, 512, 256, 4
+FLOPS = 2 * M * L * (K + H)
+
+F32 = mybir.dt.float32
+BF16 = mybir.dt.bfloat16
+U32 = mybir.dt.uint32
+U8 = mybir.dt.uint8
+E4M3X4 = mybir.dt.float8_e4m3fn_x4
+E5M2X4 = mybir.dt.float8_e5m2_x4
+ACT = mybir.ActivationFunctionType
+ALU = mybir.AluOpType
+
+P = 128
+W = 512
+SHRINK = 2.0 ** -20
+WARM = 10
+
+
+def tile_spectral_upsampling_contrast_s2_kernel(tc, low, basis_low, high, basis_high, weights, out):
+    nc = tc.nc
+    with ExitStack() as ctx:
+        keep = ctx.enter_context(tc.tile_pool(name="keep", bufs=1))
+        grp = ctx.enter_context(tc.tile_pool(name="grp", bufs=8))
+        work = ctx.enter_context(tc.tile_pool(name="work", bufs=4))
+        vals = ctx.enter_context(tc.tile_pool(name="vals", bufs=10))
+        zps = ctx.enter_context(tc.psum_pool(name="zps", bufs=5))
+        tps = ctx.enter_context(tc.psum_pool(name="tps", bufs=3))
+        ctx.enter_context(tc.manual_schedule())
+
+        low_v = low.rearrange("(g p j) (b w) -> g b p j w", p=P, j=4, w=W)
+        bl_v = basis_low.rearrange("(g p j) (h w) -> g h p j w", p=P, j=4, w=W)
+        high_v = high.rearrange("(b a p) k -> b p a k", p=P, a=4)
+        bh_v = basis_high.rearrange("(h m t) k -> h m t k", m=P, t=4)
+        out_v = out.rearrange("(b s p) (h n) -> b h p s n", p=P, s=4, n=P)
+
+        raw, gtile, codes, scales = {}, {}, {}, {}
+
+        def load(key, src):
+            raw[key] = keep.tile([P, 4, W], BF16, name="raw_" + key, align_bytes=64)
+            nc.sync.dma_start(out=raw[key][:], in_=src)
+
+        def load_key(key):
+            kind = key[:2]
+            if kind == "bl":
+                load(key, bl_v[int(key[2]), int(key[3])])
+            elif kind == "lo":
+                load(key, low_v[int(key[2]), int(key[3])])
+            elif kind == "bh":
+                load(key, bh_v[int(key[2])])
+            else:
+                load(key, high_v[int(key[2])])
+
+        ident = keep.tile([P, P], F32, name="ident")
+        make_identity(nc, ident[:])
+        w_raw = keep.tile([P, 2, J], BF16, name="w_raw")
+        w_col = keep.tile([P, 2, J], F32, name="w_col")
+        bias = keep.tile([P, 1], F32, name="bias")
+        dummy = keep.tile([P, 1], F32, name="dummy")
+        nc.vector.memset(bias[:], SHRINK * SHRINK)
+        nc.scalar.activation(out=dummy[:], in_=bias[:], func=ACT.Abs_reciprocal_sqrt, bias=bias[:])
+        nc.scalar.dma_start(out=w_raw[:], in_=weights.rearrange("(h p) j -> p h j", p=P))
+
+        for key in ["bl00","lo00","bh0","hi0","lo10","bl10","bh1","bl01","bl11","lo01","hi1","lo11","hi2","lo02","lo12","hi3","lo03","lo13"]:
+            load_key(key)
+
+        zeros = keep.tile([P, W], BF16, name="zeros")
+        nc.gpsimd.memset(zeros[:], 0.0)
+
+        def warm(n):
+            bank = zps.tile([P, W], F32, name="z")
+            for k in range(n):
+                nc.tensor.matmul(bank[:], lhsT=zeros[:, :P], rhs=zeros[:], start=True, stop=True)
+
+        warm(WARM)
+        nc.vector.tensor_scalar_mul(w_col[:], w_raw[:], SHRINK)
+
+        def group_tile(key):
+            if key not in gtile:
+                gtile[key] = grp.tile([P, 4 * W], BF16, name="g", align_bytes=64)
+            return gtile[key]
+
+        def il(eng, key, lo, hi):
+            g = group_tile(key)
+            src = raw[key]
+            if key[:2] == "bl":
+                t0, t1 = lo // P, hi // P
+                dst = g[:, 4 * lo : 4 * hi].rearrange("p (t m j) -> p t m j", m=P, j=4)
+                view = src[:].rearrange("p j (m t) -> p t m j", t=4)[:, t0:t1]
+            else:
+                dst = g[:, 4 * lo : 4 * hi].rearrange("p (c i t) -> p c t i", i=4, t=4)
+                view = src[:, :, lo:hi].rearrange("p t (c i) -> p c t i", i=4)
+            if eng == "v":
+                nc.vector.tensor_copy(out=dst, in_=view)
+            else:
+                nc.scalar.copy(out=dst, in_=view)
+
+        def quant(key):
+            codes[key] = keep.tile([P, W], U32, name="c_" + key, align_bytes=64)
+            scales[key] = keep.tile([P, W], U8, name="s_" + key, align_bytes=64)
+            x4 = E5M2X4 if key[:2] == "hi" else E4M3X4
+            nc.vector.quantize_mx(out=codes[key][:].bitcast(x4), scales=scales[key][:], in_=gtile[key][:])
+
+        def quant_part(key, lo, hi):
+            if lo == 0:
+                codes[key] = keep.tile([P, W], U32, name="c_" + key, align_bytes=64)
+                scales[key] = keep.tile([P, W], U8, name="s_" + key, align_bytes=64)
+            nc.vector.quantize_mx(out=codes[key][:, lo:hi].bitcast(E4M3X4), scales=scales[key][:, lo:hi],
+                                  in_=gtile[key][:, 4 * lo : 4 * hi])
+
+        tbank = {}
+
+        def xp(key):
+            words = raw[key][:].bitcast(F32)
+            for half in range(2):
+                bank = tps.tile([P, 4, P], F32, name="tb")
+                tbank[key, half] = bank
+                for l in range(2):
+                    for u in range(2):
+                        nc.tensor.transpose(bank[:, 2 * l + u, :], words[:, 2 * half + l, u : 256 : 2], ident[:])
+
+        def xexit(eng, key, half):
+            g = group_tile(key)
+            dst = g[:].bitcast(F32)[:, W * half : W * half + W].rearrange("p (l r u) -> p l r u", l=2, u=2)
+            src = tbank[key, half][:].rearrange("p (l u) r -> p l r u", u=2)
+            if eng == "v":
+                nc.vector.tensor_copy(out=dst, in_=src)
+            else:
+                nc.scalar.copy(out=dst, in_=src)
+
+        z, q, r, v = {}, {}, {}, {}
+
+        def one_pass(i, which, start, stop):
+            b, h, j = i // 8, (i // 4) % 2, i % 4
+            if start:
+                z[i] = zps.tile([P, W], F32, name="z")
+            cols = slice(P * j, P * j + P)
+            if which == 2:
+                wk, xk, x4 = "bh" + str(h), "hi" + str(b), E5M2X4
+            else:
+                wk, xk, x4 = "bl" + str(which) + str(h), "lo" + str(which) + str(b), E4M3X4
+            nc.tensor.matmul_mx(
+                out=z[i][:],
+                lhsT=codes[wk][:, cols].bitcast(E4M3X4),
+                lhsT_scale=scales[wk][:, cols],
+                rhs=codes[xk][:].bitcast(x4),
+                rhs_scale=scales[xk][:],
+                start=start,
+                stop=stop,
+            )
+
+        def mx(i):
+            one_pass(i, 0, True, False)
+            one_pass(i, 1, False, False)
+            one_pass(i, 2, False, True)
+
+        def sq(i):
+            q[i] = work.tile([P, W], F32, name="q")
+            nc.scalar.activation(out=q[i][:], in_=z[i][:], func=ACT.Square, scale=SHRINK)
+
+        def ars(i):
+            r[i] = work.tile([P, W], F32, name="r")
+            nc.scalar.activation(out=r[i][:], in_=q[i][:], func=ACT.Abs_reciprocal_sqrt, bias=bias[:])
+
+        def stt(i):
+            h, j = (i // 4) % 2, i % 4
+            v[i] = vals.tile([P, W], F32, name="v")
+            nc.vector.scalar_tensor_tensor(out=v[i][:], in0=z[i][:], scalar=w_col[:, h, j : j + 1], in1=r[i][:],
+                                           op0=ALU.mult, op1=ALU.mult)
+
+        def out_t(g):
+            bank = tps.tile([P, 4, P], F32, name="tb")
+            tbank[g] = bank
+            for s in range(4):
+                for j in range(J):
+                    nc.tensor.matmul(bank[:, s, :], lhsT=v[4 * g + j][:, P * s : P * s + P], rhs=ident[:],
+                                     is_transpose=True, start=(j == 0), stop=(j == J - 1))
+
+        def out_exit(eng, g):
+            o = work.tile([P, 4, P], F32, name="o")
+            if eng == "v":
+                nc.vector.tensor_copy(out=o[:], in_=tbank[g][:])
+            else:
+                nc.scalar.copy(out=o[:], in_=tbank[g][:])
+            nc.sync.dma_start(out=out_v[g // 2, g % 2], in_=o[:])
+
+
+        def sq_part(i, c0, c1):
+            if c0 == 0:
+                q[i] = work.tile([P, W], F32, name="q")
+                r[i] = work.tile([P, W], F32, name="r")
+                v[i] = vals.tile([P, W], F32, name="v")
+            nc.scalar.activation(out=q[i][:, c0:c1], in_=z[i][:, c0:c1], func=ACT.Square, scale=SHRINK)
+
+        def ars_part(i, c0, c1):
+            nc.scalar.activation(out=r[i][:, c0:c1], in_=q[i][:, c0:c1], func=ACT.Abs_reciprocal_sqrt, bias=bias[:])
+
+        def stt_part(i, c0, c1):
+            h, j = (i // 4) % 2, i % 4
+            nc.vector.scalar_tensor_tensor(out=v[i][:, c0:c1], in0=z[i][:, c0:c1], scalar=w_col[:, h, j : j + 1],
+                                           in1=r[i][:, c0:c1], op0=ALU.mult, op1=ALU.mult)
+
+        last = {}
+
+        def last_t(j, s):
+            if j == 0:
+                if s < 3:
+                    last[s] = tps.tile([P, P], F32, name="tb")
+                else:
+                    last[s] = zps.tile([P, P], F32, name="z")
+            nc.tensor.matmul(last[s][:], lhsT=v[28 + j][:, P * s : P * s + P], rhs=ident[:],
+                             is_transpose=True, start=(j == 0), stop=(j == J - 1))
+
+        il("v", "bl00", 0, 384)
+        il("s", "bl00", 384, 512)
+        quant("bl00")
+        il("v", "lo00", 0, 320)
+        il("s", "lo00", 320, 512)
+        quant("lo00")
+        xp("bh0")
+        xexit("s", "bh0", 0)
+        xexit("s", "bh0", 1)
+        for i in range(4):
+            one_pass(i, 0, True, False)
+        xp("hi0")
+        quant("bh0")
+        il("v", "lo10", 0, 320)
+        il("s", "lo10", 320, 512)
+        xexit("s", "hi0", 0)
+        xexit("s", "hi0", 1)
+        il("v", "bl10", 0, 384)
+        quant("lo10")
+        il("s", "bl10", 384, 512)
+        xp("bh1")
+        quant("hi0")
+        for i in range(4):
+            one_pass(i, 2, False, False)
+        quant_part("bl10", 0, 256)
+        one_pass(0, 1, False, True)
+        one_pass(1, 1, False, True)
+        quant_part("bl10", 256, 512)
+        one_pass(2, 1, False, True)
+        one_pass(3, 1, False, True)
+        xexit("s", "bh1", 0)
+        xexit("s", "bh1", 1)
+        il("v", "bl01", 0, 512)
+        quant("bh1")
+        il("v", "bl11", 0, 512)
+        quant("bl01")
+        quant("bl11")
+
+        v_extra = {
+            3: [(il, "v", "lo01", 0, 512)],
+            4: [(quant, "lo01"), (il, "v", "lo11", 0, 512)],
+            5: [(quant, "lo11")],
+            7: [(quant, "hi1")],
+            8: [(out_exit, "v", 0)],
+            9: [(il, "v", "lo02", 0, 512)],
+            10: [(quant, "lo02")],
+            11: [(il, "v", "lo12", 0, 512)],
+            12: [(quant, "lo12"), (out_exit, "v", 1)],
+            14: [(quant, "hi2")],
+            16: [(out_exit, "v", 2)],
+            17: [(il, "v", "lo03", 0, 512)],
+            18: [(quant, "lo03")],
+            19: [(il, "v", "lo13", 0, 512)],
+            20: [(quant, "lo13"), (out_exit, "v", 3)],
+            22: [(quant, "hi3")],
+            24: [(out_exit, "v", 4)],
+            28: [(out_exit, "v", 5)],
+        }
+        s_extra = {
+            6: [(xexit, "s", "hi1", 0), (xexit, "s", "hi1", 1)],
+            12: [(xexit, "s", "hi2", 0)],
+            13: [(xexit, "s", "hi2", 1)],
+            20: [(xexit, "s", "hi3", 0)],
+            21: [(xexit, "s", "hi3", 1)],
+        }
+        pe_extra = {
+            6: [(xp, "hi1")],
+            7: [(out_t, 0)],
+            9: [(xp, "hi2")],
+            11: [(out_t, 1)],
+            15: [(out_t, 2)],
+            17: [(xp, "hi3")],
+            19: [(out_t, 3)],
+            23: [(out_t, 4)],
+            27: [(out_t, 5)],
+            31: [(out_t, 6)],
+        }
+
+        def run(calls):
+            for call in calls:
+                call[0](*call[1:])
+
+        for i in range(32):
+            if i >= 4:
+                mx(i)
+            run(pe_extra.get(i, []))
+            if i < 31:
+                sq(i)
+            if i >= 1:
+                ars(i - 1)
+            run(s_extra.get(i, []))
+            if i >= 2:
+                stt(i - 2)
+            run(v_extra.get(i, []))
+        sq_part(31, 0, 256)
+        ars_part(31, 0, 256)
+        sq_part(31, 256, 512)
+        ars_part(31, 256, 512)
+        out_exit("v", 6)
+        stt(30)
+        for j in range(3):
+            for s in range(4):
+                last_t(j, s)
+        o = work.tile([P, 4, P], F32, name="o")
+        for s in range(4):
+            if s % 2 == 0:
+                stt_part(31, 128 * s, 128 * s + 256)
+                last_t(3, s)
+                last_t(3, s + 1)
+        for s in range(4):
+            if s % 2 == 0:
+                nc.vector.tensor_copy(out=o[:, s, :], in_=last[s][:])
+            else:
+                nc.scalar.copy(out=o[:, s, :], in_=last[s][:])
+            if s % 2 == 1:
+                nc.sync.dma_start(out=out_v[3, 1][:, s - 1 : s + 1, :], in_=o[:, s - 1 : s + 1, :])

@@ -17,317 +17,371 @@ ALU = mybir.AluOpType
 
 P = 128
 W = 512
-SHRINK = 2.0 ** -20
-WARM = 10
+PACK = 4
+UNITS = (M // W) * (B // P) * J
+GROUPS = UNITS // J
+
+SHRINK = 2.0**-20
+
+WARM_UP = 10
+Z_BANKS = 6
+
+
+def basis_low_chunk(k_pass, half):
+    return ("basis_low", k_pass, half)
+
+
+def low_chunk(k_pass, block):
+    return ("low", k_pass, block)
+
+
+def basis_high_chunk(half):
+    return ("basis_high", 2, half)
+
+
+def high_chunk(block):
+    return ("high", 2, block)
+
+
+LOADS = [
+    high_chunk(0),
+    basis_high_chunk(0),
+    low_chunk(0, 0),
+    low_chunk(1, 0),
+    basis_low_chunk(0, 0),
+    basis_low_chunk(1, 0),
+    basis_low_chunk(0, 1),
+    basis_high_chunk(1),
+    basis_low_chunk(1, 1),
+    high_chunk(1),
+    low_chunk(1, 1),
+    low_chunk(0, 1),
+    high_chunk(2),
+    high_chunk(3),
+    low_chunk(1, 2),
+    low_chunk(1, 3),
+    low_chunk(0, 3),
+    low_chunk(0, 2),
+]
+
+HEAD = [
+    ("transpose_words", high_chunk(0), 1),
+    ("transpose_words", basis_high_chunk(0), 0),
+    ("copy_words", "scalar", high_chunk(0), 1),
+    ("copy_words", "scalar", basis_high_chunk(0), 0),
+    ("interleave", "vector", low_chunk(0, 0)),
+    ("transpose_words", high_chunk(0), 0),
+    ("transpose_words", basis_high_chunk(0), 1),
+    ("copy_words", "scalar", high_chunk(0), 0),
+    ("copy_words", "scalar", basis_high_chunk(0), 1),
+    ("interleave", "scalar", low_chunk(1, 0)),
+    ("interleave", "scalar", basis_low_chunk(1, 0)),
+    ("quantise", high_chunk(0)),
+    ("quantise", basis_high_chunk(0)),
+    ("interleave", "vector", basis_low_chunk(0, 0)),
+    ("quantise", low_chunk(0, 0)),
+    ("quantise", basis_low_chunk(0, 0)),
+    ("quantise", low_chunk(1, 0)),
+    ("interleave", "vector", basis_low_chunk(0, 1)),
+    ("quantise", basis_low_chunk(1, 0)),
+    ("quantise", basis_low_chunk(0, 1)),
+    ("first_group_pass", 2),
+    ("first_group_pass", 0),
+    ("transpose_words", basis_high_chunk(1), 1),
+    ("transpose_words", basis_high_chunk(1), 0),
+    ("first_group_pass", 1),
+    ("copy_words", "scalar", basis_high_chunk(1), 1),
+    ("copy_words", "vector", basis_high_chunk(1), 0),
+    ("interleave", "vector", basis_low_chunk(1, 1)),
+    ("quantise", basis_high_chunk(1)),
+    ("quantise", basis_low_chunk(1, 1)),
+]
+
+TENSOR_STEP = {
+    0: [("transpose_words", high_chunk(1), 1), ("transpose_words", high_chunk(1), 0)],
+    5: [("transpose_words", high_chunk(2), 1)],
+    6: [("transpose_words", high_chunk(3), 1)],
+    11: [("transpose_words", high_chunk(2), 0), ("turn_group", 0)],
+    14: [("transpose_words", high_chunk(3), 0)],
+    18: [("turn_group", 1)],
+    22: [("turn_group", 2)],
+    27: [("turn_group", 3)],
+    30: [("turn_group", 4), ("turn_group", 5)],
+    31: [("turn_group", 6)],
+}
+
+SCALAR_STEP = {
+    3: [("copy_words", "scalar", high_chunk(1), 1), ("copy_words", "scalar", high_chunk(1), 0)],
+    6: [("copy_words", "scalar", high_chunk(3), 1)],
+    11: [("copy_words", "scalar", high_chunk(2), 0)],
+    30: [("store_group", "scalar", 4)],
+}
+
+VECTOR_STEP = {
+    2: [
+        ("interleave", "vector", low_chunk(1, 1)),
+        ("interleave", "vector", low_chunk(0, 1)),
+        ("quantise", low_chunk(1, 1)),
+    ],
+    3: [("quantise", low_chunk(0, 1)), ("quantise", high_chunk(1))],
+    6: [("copy_words", "vector", high_chunk(2), 1), ("interleave", "vector", low_chunk(1, 2))],
+    9: [("quantise", low_chunk(1, 2)), ("interleave", "vector", low_chunk(0, 2))],
+    12: [("quantise", low_chunk(0, 2)), ("quantise", high_chunk(2))],
+    14: [("store_group", "vector", 0), ("interleave", "vector", low_chunk(0, 3))],
+    15: [("copy_words", "vector", high_chunk(3), 0)],
+    17: [("interleave", "vector", low_chunk(1, 3))],
+    18: [("quantise", low_chunk(1, 3))],
+    19: [("quantise", low_chunk(0, 3)), ("quantise", high_chunk(3))],
+    22: [("store_group", "vector", 1)],
+    26: [("store_group", "vector", 2)],
+    27: [("store_group", "vector", 3)],
+    30: [("store_group", "vector", 5)],
+    31: [("store_group", "vector", 6)],
+}
+
+GPSIMD_STEP = {
+    4: [("add_values", 2, 3)],
+    6: [("add_values", 4, 5)],
+    8: [("add_values", 6, 7)],
+    11: [("add_values", 8, 10)],
+    14: [("add_values", 12, 13)],
+    16: [("add_values", 14, 15)],
+    18: [("add_values", 16, 17)],
+    19: [("add_values", 16, 18)],
+    24: [("add_values", 22, 23)],
+    26: [("add_values", 24, 25)],
+    27: [("add_values", 24, 26)],
+    30: [("add_values", 28, 29)],
+}
 
 
 def tile_spectral_upsampling_contrast_s2_kernel(tc, low, basis_low, high, basis_high, weights, out):
     nc = tc.nc
     with ExitStack() as ctx:
         keep = ctx.enter_context(tc.tile_pool(name="keep", bufs=1))
-        grp = ctx.enter_context(tc.tile_pool(name="grp", bufs=8))
-        work = ctx.enter_context(tc.tile_pool(name="work", bufs=4))
-        vals = ctx.enter_context(tc.tile_pool(name="vals", bufs=10))
-        zps = ctx.enter_context(tc.psum_pool(name="zps", bufs=5))
-        tps = ctx.enter_context(tc.psum_pool(name="tps", bufs=3))
+        squares = ctx.enter_context(tc.tile_pool(name="squares", bufs=4))
+        roots = ctx.enter_context(tc.tile_pool(name="roots", bufs=5))
+        values = ctx.enter_context(tc.tile_pool(name="values", bufs=11))
+        stage = ctx.enter_context(tc.tile_pool(name="stage", bufs=3))
+        z_banks = ctx.enter_context(tc.psum_pool(name="z_banks", bufs=Z_BANKS))
+        turn_banks = ctx.enter_context(tc.psum_pool(name="turn_banks", bufs=8 - Z_BANKS))
         ctx.enter_context(tc.manual_schedule())
 
-        low_v = low.rearrange("(g p j) (b w) -> g b p j w", p=P, j=4, w=W)
-        bl_v = basis_low.rearrange("(g p j) (h w) -> g h p j w", p=P, j=4, w=W)
-        high_v = high.rearrange("(b a p) k -> b p a k", p=P, a=4)
-        bh_v = basis_high.rearrange("(h m t) k -> h m t k", m=P, t=4)
-        out_v = out.rearrange("(b s p) (h n) -> b h p s n", p=P, s=4, n=P)
+        sources = {
+            "low": low.rearrange("(g p t) (b c) -> g b p t c", p=P, t=PACK, c=W),
+            "basis_low": basis_low.rearrange("(g p t) (h c) -> g h p t c", p=P, t=PACK, c=W),
+            "high": high.rearrange("(b a p) k -> b p a k", a=4, p=P),
+            "basis_high": basis_high.rearrange("(h m j) k -> h m j k", m=P, j=J),
+        }
+        out_view = out.rearrange("(b s p) (h n) -> b h p s n", s=4, p=P, n=P)
 
-        raw, gtile, codes, scales = {}, {}, {}, {}
-
-        def load(key, src):
-            raw[key] = keep.tile([P, 4, W], BF16, name="raw_" + key, align_bytes=64)
-            nc.sync.dma_start(out=raw[key][:], in_=src)
-
-        def load_key(key):
-            kind = key[:2]
-            if kind == "bl":
-                load(key, bl_v[int(key[2]), int(key[3])])
-            elif kind == "lo":
-                load(key, low_v[int(key[2]), int(key[3])])
-            elif kind == "bh":
-                load(key, bh_v[int(key[2])])
-            else:
-                load(key, high_v[int(key[2])])
-
-        ident = keep.tile([P, P], F32, name="ident")
-        make_identity(nc, ident[:])
-        w_raw = keep.tile([P, 2, J], BF16, name="w_raw")
-        w_col = keep.tile([P, 2, J], F32, name="w_col")
-        bias = keep.tile([P, 1], F32, name="bias")
-        dummy = keep.tile([P, 1], F32, name="dummy")
-        nc.vector.memset(bias[:], SHRINK * SHRINK)
-        nc.scalar.activation(out=dummy[:], in_=bias[:], func=ACT.Abs_reciprocal_sqrt, bias=bias[:])
-        nc.scalar.dma_start(out=w_raw[:], in_=weights.rearrange("(h p) j -> p h j", p=P))
-
-        for key in ["bl00","lo00","bh0","hi0","lo10","bl10","bh1","bl01","bl11","lo01","hi1","lo11","hi2","lo02","lo12","hi3","lo03","lo13"]:
-            load_key(key)
-
+        identity = keep.tile([P, P], F32, name="identity")
+        make_identity(nc, identity[:])
+        weights_raw = keep.tile([P, 2, J], BF16, name="weights_raw")
+        weights_scaled = keep.tile([P, 2, J], F32, name="weights_scaled")
+        one = keep.tile([P, 1], F32, name="one")
+        preload = keep.tile([P, 1], F32, name="preload")
         zeros = keep.tile([P, W], BF16, name="zeros")
+        nc.vector.memset(one[:], SHRINK * SHRINK)
+        nc.scalar.activation(out=preload[:], in_=one[:], func=ACT.Abs_reciprocal_sqrt, bias=one[:])
+        nc.scalar.dma_start(out=weights_raw[:], in_=weights.rearrange("(h p) j -> p h j", p=P))
+
+        raw = {}
+        for chunk in LOADS:
+            operand, k_pass, part = chunk
+            source = sources[operand][part] if operand in ("high", "basis_high") else sources[operand][k_pass, part]
+            raw[chunk] = keep.tile([P, 4, W], BF16, name="raw_%s_%d_%d" % chunk, align_bytes=64)
+            nc.sync.dma_start(out=raw[chunk][:], in_=source)
+
         nc.gpsimd.memset(zeros[:], 0.0)
+        warm_bank = z_banks.tile([P, W], F32, name="z")
+        for repeat in range(WARM_UP):
+            nc.tensor.matmul(warm_bank[:], lhsT=zeros[:, :P], rhs=zeros[:], start=True, stop=True)
+        nc.gpsimd.tensor_scalar_mul(weights_scaled[:], weights_raw[:], SHRINK)
 
-        def warm(n):
-            bank = zps.tile([P, W], F32, name="z")
-            for k in range(n):
-                nc.tensor.matmul(bank[:], lhsT=zeros[:, :P], rhs=zeros[:], start=True, stop=True)
+        grouped, codes, scales, turned = {}, {}, {}, {}
 
-        warm(WARM)
-        nc.vector.tensor_scalar_mul(w_col[:], w_raw[:], SHRINK)
+        def grouped_tile(chunk):
+            if chunk not in grouped:
+                grouped[chunk] = keep.tile([P, W * PACK], BF16, name="grouped_%s_%d_%d" % chunk, align_bytes=64)
+            return grouped[chunk]
 
-        def group_tile(key):
-            if key not in gtile:
-                gtile[key] = grp.tile([P, 4 * W], BF16, name="g", align_bytes=64)
-            return gtile[key]
-
-        def il(eng, key, lo, hi):
-            g = group_tile(key)
-            src = raw[key]
-            if key[:2] == "bl":
-                t0, t1 = lo // P, hi // P
-                dst = g[:, 4 * lo : 4 * hi].rearrange("p (t m j) -> p t m j", m=P, j=4)
-                view = src[:].rearrange("p j (m t) -> p t m j", t=4)[:, t0:t1]
+        def interleave(engine, chunk):
+            copy = nc.vector.tensor_copy if engine == "vector" else nc.scalar.copy
+            if chunk[0] == "low":
+                copy(
+                    out=grouped_tile(chunk)[:].rearrange("p (c i t) -> p c t i", i=4, t=PACK),
+                    in_=raw[chunk][:].rearrange("p t (c i) -> p c t i", i=4),
+                )
             else:
-                dst = g[:, 4 * lo : 4 * hi].rearrange("p (c i t) -> p c t i", i=4, t=4)
-                view = src[:, :, lo:hi].rearrange("p t (c i) -> p c t i", i=4)
-            if eng == "v":
-                nc.vector.tensor_copy(out=dst, in_=view)
+                js_at_once = 2 if engine == "vector" else J
+                for j in range(0, J, js_at_once):
+                    js = slice(j, j + js_at_once)
+                    copy(
+                        out=grouped_tile(chunk)[:].rearrange("p (j m t) -> p m j t", j=J, t=PACK)[:, :, js],
+                        in_=raw[chunk][:].rearrange("p t (m j) -> p m j t", j=J)[:, :, js],
+                    )
+
+        def transpose_words(chunk, half):
+            words = raw[chunk][:].bitcast(F32)
+            bank = turn_banks.tile([P, 4, P], F32, name="turned")
+            turned[chunk, half] = bank
+            for a in range(2):
+                for u in range(2):
+                    nc.tensor.transpose(bank[:, 2 * a + u, :], words[:, 2 * half + a, u : 2 * P : 2], identity[:])
+
+        def copy_words(engine, chunk, half):
+            words = grouped_tile(chunk)[:].bitcast(F32)[:, W * half : W * (half + 1)]
+            target = words.rearrange("p (a c u) -> p a c u", a=2, u=2)
+            source = turned[chunk, half][:].rearrange("p (a u) c -> p a c u", u=2)
+            if engine == "vector":
+                nc.vector.tensor_copy(out=target, in_=source)
             else:
-                nc.scalar.copy(out=dst, in_=view)
+                nc.scalar.copy(out=target, in_=source)
 
-        def quant(key):
-            codes[key] = keep.tile([P, W], U32, name="c_" + key, align_bytes=64)
-            scales[key] = keep.tile([P, W], U8, name="s_" + key, align_bytes=64)
-            x4 = E5M2X4 if key[:2] == "hi" else E4M3X4
-            nc.vector.quantize_mx(out=codes[key][:].bitcast(x4), scales=scales[key][:], in_=gtile[key][:])
+        def quantise(chunk):
+            codes[chunk] = keep.tile([P, W], U32, name="codes_%s_%d_%d" % chunk, align_bytes=64)
+            scales[chunk] = keep.tile([P, W], U8, name="scales_%s_%d_%d" % chunk, align_bytes=64)
+            packed = E5M2X4 if chunk[0] == "high" else E4M3X4
+            nc.vector.quantize_mx(out=codes[chunk][:].bitcast(packed), scales=scales[chunk][:], in_=grouped[chunk][:])
 
-        def quant_part(key, lo, hi):
-            if lo == 0:
-                codes[key] = keep.tile([P, W], U32, name="c_" + key, align_bytes=64)
-                scales[key] = keep.tile([P, W], U8, name="s_" + key, align_bytes=64)
-            nc.vector.quantize_mx(out=codes[key][:, lo:hi].bitcast(E4M3X4), scales=scales[key][:, lo:hi],
-                                  in_=gtile[key][:, 4 * lo : 4 * hi])
+        z, square_of, root, value = {}, {}, {}, {}
+        passes_done = {i: 0 for i in range(UNITS)}
 
-        tbank = {}
-
-        def xp(key):
-            words = raw[key][:].bitcast(F32)
-            for half in range(2):
-                bank = tps.tile([P, 4, P], F32, name="tb")
-                tbank[key, half] = bank
-                for l in range(2):
-                    for u in range(2):
-                        nc.tensor.transpose(bank[:, 2 * l + u, :], words[:, 2 * half + l, u : 256 : 2], ident[:])
-
-        def xexit(eng, key, half):
-            g = group_tile(key)
-            dst = g[:].bitcast(F32)[:, W * half : W * half + W].rearrange("p (l r u) -> p l r u", l=2, u=2)
-            src = tbank[key, half][:].rearrange("p (l u) r -> p l r u", u=2)
-            if eng == "v":
-                nc.vector.tensor_copy(out=dst, in_=src)
+        def one_pass(i, k_pass):
+            block, half, j = i // 8, (i // 4) % 2, i % 4
+            if k_pass == 2:
+                base, pixels, packed = basis_high_chunk(half), high_chunk(block), E5M2X4
             else:
-                nc.scalar.copy(out=dst, in_=src)
-
-        z, q, r, v = {}, {}, {}, {}
-
-        def one_pass(i, which, start, stop):
-            b, h, j = i // 8, (i // 4) % 2, i % 4
-            if start:
-                z[i] = zps.tile([P, W], F32, name="z")
-            cols = slice(P * j, P * j + P)
-            if which == 2:
-                wk, xk, x4 = "bh" + str(h), "hi" + str(b), E5M2X4
-            else:
-                wk, xk, x4 = "bl" + str(which) + str(h), "lo" + str(which) + str(b), E4M3X4
+                base, pixels, packed = basis_low_chunk(k_pass, half), low_chunk(k_pass, block), E4M3X4
+            if passes_done[i] == 0:
+                z[i] = z_banks.tile([P, W], F32, name="z")
+            passes_done[i] += 1
+            columns = slice(P * j, P * (j + 1))
             nc.tensor.matmul_mx(
                 out=z[i][:],
-                lhsT=codes[wk][:, cols].bitcast(E4M3X4),
-                lhsT_scale=scales[wk][:, cols],
-                rhs=codes[xk][:].bitcast(x4),
-                rhs_scale=scales[xk][:],
-                start=start,
-                stop=stop,
+                lhsT=codes[base][:, columns].bitcast(E4M3X4),
+                lhsT_scale=scales[base][:, columns],
+                rhs=codes[pixels][:].bitcast(packed),
+                rhs_scale=scales[pixels][:],
+                start=(passes_done[i] == 1),
+                stop=(passes_done[i] == 3),
             )
 
-        def mx(i):
-            one_pass(i, 0, True, False)
-            one_pass(i, 1, False, False)
-            one_pass(i, 2, False, True)
+        def first_group_pass(k_pass):
+            for i in range(J):
+                one_pass(i, k_pass)
 
-        def sq(i):
-            q[i] = work.tile([P, W], F32, name="q")
-            nc.scalar.activation(out=q[i][:], in_=z[i][:], func=ACT.Square, scale=SHRINK)
+        def square(i, start=0, stop=W):
+            if start == 0:
+                square_of[i] = squares.tile([P, W], F32, name="square")
+            nc.scalar.activation(
+                out=square_of[i][:, start:stop],
+                in_=z[i][:, start:stop],
+                func=ACT.Square,
+                scale=SHRINK,
+            )
 
-        def ars(i):
-            r[i] = work.tile([P, W], F32, name="r")
-            nc.scalar.activation(out=r[i][:], in_=q[i][:], func=ACT.Abs_reciprocal_sqrt, bias=bias[:])
+        def reciprocal_root(i, start=0, stop=W):
+            if start == 0:
+                root[i] = roots.tile([P, W], F32, name="root")
+            nc.scalar.activation(
+                out=root[i][:, start:stop],
+                in_=square_of[i][:, start:stop],
+                func=ACT.Abs_reciprocal_sqrt,
+                bias=one[:],
+            )
 
-        def stt(i):
-            h, j = (i // 4) % 2, i % 4
-            v[i] = vals.tile([P, W], F32, name="v")
-            nc.vector.scalar_tensor_tensor(out=v[i][:], in0=z[i][:], scalar=w_col[:, h, j : j + 1], in1=r[i][:],
-                                           op0=ALU.mult, op1=ALU.mult)
+        def weigh(i, start=0, stop=W):
+            half, j = (i // 4) % 2, i % 4
+            if start == 0:
+                value[i] = values.tile([P, W], F32, name="value")
+            nc.vector.scalar_tensor_tensor(
+                out=value[i][:, start:stop],
+                in0=z[i][:, start:stop],
+                scalar=weights_scaled[:, half, j : j + 1],
+                in1=root[i][:, start:stop],
+                op0=ALU.mult,
+                op1=ALU.mult,
+            )
 
-        def out_t(g):
-            bank = tps.tile([P, 4, P], F32, name="tb")
-            tbank[g] = bank
+        left = {g: list(range(J * g, J * (g + 1))) for g in range(GROUPS)}
+
+        def add_values(i, other):
+            nc.gpsimd.tensor_tensor(out=value[i][:], in0=value[i][:], in1=value[other][:], op=ALU.add)
+            left[i // J].remove(other)
+
+        def turn_and_add(bank, i, s, first, last):
+            nc.tensor.matmul(bank, lhsT=value[i][:, P * s : P * (s + 1)], rhs=identity[:], is_transpose=True,
+                             start=first, stop=last)
+
+        def turn_group(g):
+            bank = turn_banks.tile([P, 4, P], F32, name="turned")
+            turned[g] = bank
             for s in range(4):
-                for j in range(J):
-                    nc.tensor.matmul(bank[:, s, :], lhsT=v[4 * g + j][:, P * s : P * s + P], rhs=ident[:],
-                                     is_transpose=True, start=(j == 0), stop=(j == J - 1))
+                for i in left[g]:
+                    turn_and_add(bank[:, s, :], i, s, i == left[g][0], i == left[g][-1])
 
-        def out_exit(eng, g):
-            o = work.tile([P, 4, P], F32, name="o")
-            if eng == "v":
-                nc.vector.tensor_copy(out=o[:], in_=tbank[g][:])
+        def store_group(engine, g):
+            result = stage.tile([P, 4, P], F32, name="result")
+            if engine == "vector":
+                nc.vector.tensor_copy(out=result[:], in_=turned[g][:])
             else:
-                nc.scalar.copy(out=o[:], in_=tbank[g][:])
-            nc.sync.dma_start(out=out_v[g // 2, g % 2], in_=o[:])
+                nc.scalar.copy(out=result[:], in_=turned[g][:])
+            nc.sync.dma_start(out=out_view[g // 2, g % 2], in_=result[:])
 
-
-        def sq_part(i, c0, c1):
-            if c0 == 0:
-                q[i] = work.tile([P, W], F32, name="q")
-                r[i] = work.tile([P, W], F32, name="r")
-                v[i] = vals.tile([P, W], F32, name="v")
-            nc.scalar.activation(out=q[i][:, c0:c1], in_=z[i][:, c0:c1], func=ACT.Square, scale=SHRINK)
-
-        def ars_part(i, c0, c1):
-            nc.scalar.activation(out=r[i][:, c0:c1], in_=q[i][:, c0:c1], func=ACT.Abs_reciprocal_sqrt, bias=bias[:])
-
-        def stt_part(i, c0, c1):
-            h, j = (i // 4) % 2, i % 4
-            nc.vector.scalar_tensor_tensor(out=v[i][:, c0:c1], in0=z[i][:, c0:c1], scalar=w_col[:, h, j : j + 1],
-                                           in1=r[i][:, c0:c1], op0=ALU.mult, op1=ALU.mult)
-
-        last = {}
-
-        def last_t(j, s):
-            if j == 0:
-                if s < 3:
-                    last[s] = tps.tile([P, P], F32, name="tb")
-                else:
-                    last[s] = zps.tile([P, P], F32, name="z")
-            nc.tensor.matmul(last[s][:], lhsT=v[28 + j][:, P * s : P * s + P], rhs=ident[:],
-                             is_transpose=True, start=(j == 0), stop=(j == J - 1))
-
-        il("v", "bl00", 0, 384)
-        il("s", "bl00", 384, 512)
-        quant("bl00")
-        il("v", "lo00", 0, 320)
-        il("s", "lo00", 320, 512)
-        quant("lo00")
-        xp("bh0")
-        xexit("s", "bh0", 0)
-        xexit("s", "bh0", 1)
-        for i in range(4):
-            one_pass(i, 0, True, False)
-        xp("hi0")
-        quant("bh0")
-        il("v", "lo10", 0, 320)
-        il("s", "lo10", 320, 512)
-        xexit("s", "hi0", 0)
-        xexit("s", "hi0", 1)
-        il("v", "bl10", 0, 384)
-        quant("lo10")
-        il("s", "bl10", 384, 512)
-        xp("bh1")
-        quant("hi0")
-        for i in range(4):
-            one_pass(i, 2, False, False)
-        quant_part("bl10", 0, 256)
-        one_pass(0, 1, False, True)
-        one_pass(1, 1, False, True)
-        quant_part("bl10", 256, 512)
-        one_pass(2, 1, False, True)
-        one_pass(3, 1, False, True)
-        xexit("s", "bh1", 0)
-        xexit("s", "bh1", 1)
-        il("v", "bl01", 0, 512)
-        quant("bh1")
-        il("v", "bl11", 0, 512)
-        quant("bl01")
-        quant("bl11")
-
-        v_extra = {
-            3: [(il, "v", "lo01", 0, 512)],
-            4: [(quant, "lo01"), (il, "v", "lo11", 0, 512)],
-            5: [(quant, "lo11")],
-            7: [(quant, "hi1")],
-            8: [(out_exit, "v", 0)],
-            9: [(il, "v", "lo02", 0, 512)],
-            10: [(quant, "lo02")],
-            11: [(il, "v", "lo12", 0, 512)],
-            12: [(quant, "lo12"), (out_exit, "v", 1)],
-            14: [(quant, "hi2")],
-            16: [(out_exit, "v", 2)],
-            17: [(il, "v", "lo03", 0, 512)],
-            18: [(quant, "lo03")],
-            19: [(il, "v", "lo13", 0, 512)],
-            20: [(quant, "lo13"), (out_exit, "v", 3)],
-            22: [(quant, "hi3")],
-            24: [(out_exit, "v", 4)],
-            28: [(out_exit, "v", 5)],
-        }
-        s_extra = {
-            6: [(xexit, "s", "hi1", 0), (xexit, "s", "hi1", 1)],
-            12: [(xexit, "s", "hi2", 0)],
-            13: [(xexit, "s", "hi2", 1)],
-            20: [(xexit, "s", "hi3", 0)],
-            21: [(xexit, "s", "hi3", 1)],
-        }
-        pe_extra = {
-            6: [(xp, "hi1")],
-            7: [(out_t, 0)],
-            9: [(xp, "hi2")],
-            11: [(out_t, 1)],
-            15: [(out_t, 2)],
-            17: [(xp, "hi3")],
-            19: [(out_t, 3)],
-            23: [(out_t, 4)],
-            27: [(out_t, 5)],
-            31: [(out_t, 6)],
+        calls = {
+            "interleave": interleave,
+            "quantise": quantise,
+            "transpose_words": transpose_words,
+            "copy_words": copy_words,
+            "first_group_pass": first_group_pass,
+            "turn_group": turn_group,
+            "store_group": store_group,
+            "add_values": add_values,
         }
 
-        def run(calls):
-            for call in calls:
-                call[0](*call[1:])
+        def run(entries):
+            for entry in entries:
+                calls[entry[0]](*entry[1:])
 
-        for i in range(32):
-            if i >= 4:
-                mx(i)
-            run(pe_extra.get(i, []))
-            if i < 31:
-                sq(i)
+        run(HEAD)
+        last_unit = UNITS - 1
+        for i in range(UNITS):
+            if i >= J:
+                for k_pass in range(3):
+                    one_pass(i, k_pass)
+            run(TENSOR_STEP.get(i, []))
+            if i < last_unit:
+                square(i)
             if i >= 1:
-                ars(i - 1)
-            run(s_extra.get(i, []))
-            if i >= 2:
-                stt(i - 2)
-            run(v_extra.get(i, []))
-        sq_part(31, 0, 256)
-        ars_part(31, 0, 256)
-        sq_part(31, 256, 512)
-        ars_part(31, 256, 512)
-        out_exit("v", 6)
-        stt(30)
-        for j in range(3):
-            for s in range(4):
-                last_t(j, s)
-        o = work.tile([P, 4, P], F32, name="o")
+                reciprocal_root(i - 1)
+            run(SCALAR_STEP.get(i, []))
+            if i >= 1:
+                weigh(i - 1)
+            run(VECTOR_STEP.get(i, []))
+            run(GPSIMD_STEP.get(i, []))
+
+        halves = ((0, W // 2), (W // 2, W))
+        for start, stop in halves:
+            square(last_unit, start, stop)
+            reciprocal_root(last_unit, start, stop)
+        slices = []
         for s in range(4):
-            if s % 2 == 0:
-                stt_part(31, 128 * s, 128 * s + 256)
-                last_t(3, s)
-                last_t(3, s + 1)
-        for s in range(4):
-            if s % 2 == 0:
-                nc.vector.tensor_copy(out=o[:, s, :], in_=last[s][:])
+            if s < 8 - Z_BANKS:
+                slices.append(turn_banks.tile([P, P], F32, name="turned"))
             else:
-                nc.scalar.copy(out=o[:, s, :], in_=last[s][:])
-            if s % 2 == 1:
-                nc.sync.dma_start(out=out_v[3, 1][:, s - 1 : s + 1, :], in_=o[:, s - 1 : s + 1, :])
+                slices.append(z_banks.tile([P, P], F32, name="z"))
+        rest = left[GROUPS - 1]
+        for i in rest[:-1]:
+            for s in range(4):
+                turn_and_add(slices[s][:], i, s, i == rest[0], False)
+        for start, stop in halves:
+            weigh(last_unit, start, stop)
+        for s in range(4):
+            turn_and_add(slices[s][:], last_unit, s, False, True)
+        result = stage.tile([P, 4, P], F32, name="result")
+        for s in range(0, 4, 2):
+            nc.vector.tensor_copy(out=result[:, s, :], in_=slices[s][:])
+            nc.scalar.copy(out=result[:, s + 1, :], in_=slices[s + 1][:])
+            nc.sync.dma_start(out=out_view[3, 1][:, s : s + 2, :], in_=result[:, s : s + 2, :])

from contextlib import ExitStack

import concourse.mybir as mybir
from concourse.masks import make_identity

M, L, K, H, B, J = 2048, 1024, 1024, 512, 256, 4
FLOPS = 2 * M * L * (K + H)

F32 = mybir.dt.float32
BF16 = mybir.dt.bfloat16
U32 = mybir.dt.uint32
U8 = mybir.dt.uint8
E4M3X4 = mybir.dt.float8_e4m3fn_x4
E5M2X4 = mybir.dt.float8_e5m2_x4
ACT = mybir.ActivationFunctionType
ALU = mybir.AluOpType

P = 128
W = 512
PACK = 4
UNITS = (M // W) * (B // P) * J
GROUPS = UNITS // J

SHRINK = 2.0**-20

WARM_UP = 10
Z_BANKS = 6


def basis_low_chunk(k_pass, half):
    return ("basis_low", k_pass, half)


def low_chunk(k_pass, block):
    return ("low", k_pass, block)


def basis_high_chunk(half):
    return ("basis_high", 2, half)


def high_chunk(block):
    return ("high", 2, block)


LOADS = [
    high_chunk(0),
    basis_high_chunk(0),
    low_chunk(0, 0),
    low_chunk(1, 0),
    basis_low_chunk(0, 0),
    basis_low_chunk(1, 0),
    basis_low_chunk(0, 1),
    basis_high_chunk(1),
    basis_low_chunk(1, 1),
    high_chunk(1),
    low_chunk(1, 1),
    low_chunk(0, 1),
    high_chunk(2),
    high_chunk(3),
    low_chunk(1, 2),
    low_chunk(1, 3),
    low_chunk(0, 3),
    low_chunk(0, 2),
]

HEAD = [
    ("transpose_words", high_chunk(0), 1),
    ("transpose_words", basis_high_chunk(0), 0),
    ("copy_words", "scalar", high_chunk(0), 1),
    ("copy_words", "scalar", basis_high_chunk(0), 0),
    ("interleave", "vector", low_chunk(0, 0)),
    ("transpose_words", high_chunk(0), 0),
    ("transpose_words", basis_high_chunk(0), 1),
    ("copy_words", "scalar", high_chunk(0), 0),
    ("copy_words", "scalar", basis_high_chunk(0), 1),
    ("interleave", "scalar", low_chunk(1, 0)),
    ("interleave", "scalar", basis_low_chunk(1, 0)),
    ("quantise", high_chunk(0)),
    ("quantise", basis_high_chunk(0)),
    ("interleave", "vector", basis_low_chunk(0, 0)),
    ("quantise", low_chunk(0, 0)),
    ("quantise", basis_low_chunk(0, 0)),
    ("quantise", low_chunk(1, 0)),
    ("interleave", "vector", basis_low_chunk(0, 1)),
    ("quantise", basis_low_chunk(1, 0)),
    ("quantise", basis_low_chunk(0, 1)),
    ("first_group_pass", 2),
    ("first_group_pass", 0),
    ("transpose_words", basis_high_chunk(1), 1),
    ("transpose_words", basis_high_chunk(1), 0),
    ("first_group_pass", 1),
    ("copy_words", "scalar", basis_high_chunk(1), 1),
    ("copy_words", "vector", basis_high_chunk(1), 0),
    ("interleave", "vector", basis_low_chunk(1, 1)),
    ("quantise", basis_high_chunk(1)),
    ("quantise", basis_low_chunk(1, 1)),
]

TENSOR_STEP = {
    0: [("transpose_words", high_chunk(1), 1), ("transpose_words", high_chunk(1), 0)],
    5: [("transpose_words", high_chunk(2), 1)],
    6: [("transpose_words", high_chunk(3), 1)],
    11: [("transpose_words", high_chunk(2), 0), ("turn_group", 0)],
    14: [("transpose_words", high_chunk(3), 0)],
    18: [("turn_group", 1)],
    22: [("turn_group", 2)],
    27: [("turn_group", 3)],
    30: [("turn_group", 4), ("turn_group", 5)],
    31: [("turn_group", 6)],
}

SCALAR_STEP = {
    3: [("copy_words", "scalar", high_chunk(1), 1), ("copy_words", "scalar", high_chunk(1), 0)],
    6: [("copy_words", "scalar", high_chunk(3), 1)],
    11: [("copy_words", "scalar", high_chunk(2), 0)],
    30: [("store_group", "scalar", 4)],
}

VECTOR_STEP = {
    2: [
        ("interleave", "vector", low_chunk(1, 1)),
        ("interleave", "vector", low_chunk(0, 1)),
        ("quantise", low_chunk(1, 1)),
    ],
    3: [("quantise", low_chunk(0, 1)), ("quantise", high_chunk(1))],
    6: [("copy_words", "vector", high_chunk(2), 1), ("interleave", "vector", low_chunk(1, 2))],
    9: [("quantise", low_chunk(1, 2)), ("interleave", "vector", low_chunk(0, 2))],
    12: [("quantise", low_chunk(0, 2)), ("quantise", high_chunk(2))],
    14: [("store_group", "vector", 0), ("interleave", "vector", low_chunk(0, 3))],
    15: [("copy_words", "vector", high_chunk(3), 0)],
    17: [("interleave", "vector", low_chunk(1, 3))],
    18: [("quantise", low_chunk(1, 3))],
    19: [("quantise", low_chunk(0, 3)), ("quantise", high_chunk(3))],
    22: [("store_group", "vector", 1)],
    26: [("store_group", "vector", 2)],
    27: [("store_group", "vector", 3)],
    30: [("store_group", "vector", 5)],
    31: [("store_group", "vector", 6)],
}

GPSIMD_STEP = {
    4: [("add_values", 2, 3)],
    6: [("add_values", 4, 5)],
    8: [("add_values", 6, 7)],
    11: [("add_values", 8, 10)],
    14: [("add_values", 12, 13)],
    16: [("add_values", 14, 15)],
    18: [("add_values", 16, 17)],
    19: [("add_values", 16, 18)],
    24: [("add_values", 22, 23)],
    26: [("add_values", 24, 25)],
    27: [("add_values", 24, 26)],
    30: [("add_values", 28, 29)],
}


def tile_spectral_upsampling_contrast_s2_kernel(tc, low, basis_low, high, basis_high, weights, out):
    nc = tc.nc
    with ExitStack() as ctx:
        keep = ctx.enter_context(tc.tile_pool(name="keep", bufs=1))
        squares = ctx.enter_context(tc.tile_pool(name="squares", bufs=4))
        roots = ctx.enter_context(tc.tile_pool(name="roots", bufs=5))
        values = ctx.enter_context(tc.tile_pool(name="values", bufs=11))
        stage = ctx.enter_context(tc.tile_pool(name="stage", bufs=3))
        z_banks = ctx.enter_context(tc.psum_pool(name="z_banks", bufs=Z_BANKS))
        turn_banks = ctx.enter_context(tc.psum_pool(name="turn_banks", bufs=8 - Z_BANKS))
        ctx.enter_context(tc.manual_schedule())

        sources = {
            "low": low.rearrange("(g p t) (b c) -> g b p t c", p=P, t=PACK, c=W),
            "basis_low": basis_low.rearrange("(g p t) (h c) -> g h p t c", p=P, t=PACK, c=W),
            "high": high.rearrange("(b a p) k -> b p a k", a=4, p=P),
            "basis_high": basis_high.rearrange("(h m j) k -> h m j k", m=P, j=J),
        }
        out_view = out.rearrange("(b s p) (h n) -> b h p s n", s=4, p=P, n=P)

        identity = keep.tile([P, P], F32, name="identity")
        make_identity(nc, identity[:])
        weights_raw = keep.tile([P, 2, J], BF16, name="weights_raw")
        weights_scaled = keep.tile([P, 2, J], F32, name="weights_scaled")
        one = keep.tile([P, 1], F32, name="one")
        preload = keep.tile([P, 1], F32, name="preload")
        zeros = keep.tile([P, W], BF16, name="zeros")
        nc.vector.memset(one[:], SHRINK * SHRINK)
        nc.scalar.activation(out=preload[:], in_=one[:], func=ACT.Abs_reciprocal_sqrt, bias=one[:])
        nc.scalar.dma_start(out=weights_raw[:], in_=weights.rearrange("(h p) j -> p h j", p=P))

        raw = {}
        for chunk in LOADS:
            operand, k_pass, part = chunk
            source = sources[operand][part] if operand in ("high", "basis_high") else sources[operand][k_pass, part]
            raw[chunk] = keep.tile([P, 4, W], BF16, name="raw_%s_%d_%d" % chunk, align_bytes=64)
            nc.sync.dma_start(out=raw[chunk][:], in_=source)

        nc.gpsimd.memset(zeros[:], 0.0)
        warm_bank = z_banks.tile([P, W], F32, name="z")
        for repeat in range(WARM_UP):
            nc.tensor.matmul(warm_bank[:], lhsT=zeros[:, :P], rhs=zeros[:], start=True, stop=True)
        nc.gpsimd.tensor_scalar_mul(weights_scaled[:], weights_raw[:], SHRINK)

        grouped, codes, scales, turned = {}, {}, {}, {}

        def grouped_tile(chunk):
            if chunk not in grouped:
                grouped[chunk] = keep.tile([P, W * PACK], BF16, name="grouped_%s_%d_%d" % chunk, align_bytes=64)
            return grouped[chunk]

        def interleave(engine, chunk):
            copy = nc.vector.tensor_copy if engine == "vector" else nc.scalar.copy
            if chunk[0] == "low":
                copy(
                    out=grouped_tile(chunk)[:].rearrange("p (c i t) -> p c t i", i=4, t=PACK),
                    in_=raw[chunk][:].rearrange("p t (c i) -> p c t i", i=4),
                )
            else:
                js_at_once = 2 if engine == "vector" else J
                for j in range(0, J, js_at_once):
                    js = slice(j, j + js_at_once)
                    copy(
                        out=grouped_tile(chunk)[:].rearrange("p (j m t) -> p m j t", j=J, t=PACK)[:, :, js],
                        in_=raw[chunk][:].rearrange("p t (m j) -> p m j t", j=J)[:, :, js],
                    )

        def transpose_words(chunk, half):
            words = raw[chunk][:].bitcast(F32)
            bank = turn_banks.tile([P, 4, P], F32, name="turned")
            turned[chunk, half] = bank
            for a in range(2):
                for u in range(2):
                    nc.tensor.transpose(bank[:, 2 * a + u, :], words[:, 2 * half + a, u : 2 * P : 2], identity[:])

        def copy_words(engine, chunk, half):
            words = grouped_tile(chunk)[:].bitcast(F32)[:, W * half : W * (half + 1)]
            target = words.rearrange("p (a c u) -> p a c u", a=2, u=2)
            source = turned[chunk, half][:].rearrange("p (a u) c -> p a c u", u=2)
            if engine == "vector":
                nc.vector.tensor_copy(out=target, in_=source)
            else:
                nc.scalar.copy(out=target, in_=source)

        def quantise(chunk):
            codes[chunk] = keep.tile([P, W], U32, name="codes_%s_%d_%d" % chunk, align_bytes=64)
            scales[chunk] = keep.tile([P, W], U8, name="scales_%s_%d_%d" % chunk, align_bytes=64)
            packed = E5M2X4 if chunk[0] == "high" else E4M3X4
            nc.vector.quantize_mx(out=codes[chunk][:].bitcast(packed), scales=scales[chunk][:], in_=grouped[chunk][:])

        z, square_of, root, value = {}, {}, {}, {}
        passes_done = {i: 0 for i in range(UNITS)}

        def one_pass(i, k_pass):
            block, half, j = i // 8, (i // 4) % 2, i % 4
            if k_pass == 2:
                base, pixels, packed = basis_high_chunk(half), high_chunk(block), E5M2X4
            else:
                base, pixels, packed = basis_low_chunk(k_pass, half), low_chunk(k_pass, block), E4M3X4
            if passes_done[i] == 0:
                z[i] = z_banks.tile([P, W], F32, name="z")
            passes_done[i] += 1
            columns = slice(P * j, P * (j + 1))
            nc.tensor.matmul_mx(
                out=z[i][:],
                lhsT=codes[base][:, columns].bitcast(E4M3X4),
                lhsT_scale=scales[base][:, columns],
                rhs=codes[pixels][:].bitcast(packed),
                rhs_scale=scales[pixels][:],
                start=(passes_done[i] == 1),
                stop=(passes_done[i] == 3),
            )

        def first_group_pass(k_pass):
            for i in range(J):
                one_pass(i, k_pass)

        def square(i, start=0, stop=W):
            if start == 0:
                square_of[i] = squares.tile([P, W], F32, name="square")
            nc.scalar.activation(
                out=square_of[i][:, start:stop],
                in_=z[i][:, start:stop],
                func=ACT.Square,
                scale=SHRINK,
            )

        def reciprocal_root(i, start=0, stop=W):
            if start == 0:
                root[i] = roots.tile([P, W], F32, name="root")
            nc.scalar.activation(
                out=root[i][:, start:stop],
                in_=square_of[i][:, start:stop],
                func=ACT.Abs_reciprocal_sqrt,
                bias=one[:],
            )

        def weigh(i, start=0, stop=W):
            half, j = (i // 4) % 2, i % 4
            if start == 0:
                value[i] = values.tile([P, W], F32, name="value")
            nc.vector.scalar_tensor_tensor(
                out=value[i][:, start:stop],
                in0=z[i][:, start:stop],
                scalar=weights_scaled[:, half, j : j + 1],
                in1=root[i][:, start:stop],
                op0=ALU.mult,
                op1=ALU.mult,
            )

        left = {g: list(range(J * g, J * (g + 1))) for g in range(GROUPS)}

        def add_values(i, other):
            nc.gpsimd.tensor_tensor(out=value[i][:], in0=value[i][:], in1=value[other][:], op=ALU.add)
            left[i // J].remove(other)

        def turn_and_add(bank, i, s, first, last):
            nc.tensor.matmul(bank, lhsT=value[i][:, P * s : P * (s + 1)], rhs=identity[:], is_transpose=True,
                             start=first, stop=last)

        def turn_group(g):
            bank = turn_banks.tile([P, 4, P], F32, name="turned")
            turned[g] = bank
            for s in range(4):
                for i in left[g]:
                    turn_and_add(bank[:, s, :], i, s, i == left[g][0], i == left[g][-1])

        def store_group(engine, g):
            result = stage.tile([P, 4, P], F32, name="result")
            if engine == "vector":
                nc.vector.tensor_copy(out=result[:], in_=turned[g][:])
            else:
                nc.scalar.copy(out=result[:], in_=turned[g][:])
            nc.sync.dma_start(out=out_view[g // 2, g % 2], in_=result[:])

        calls = {
            "interleave": interleave,
            "quantise": quantise,
            "transpose_words": transpose_words,
            "copy_words": copy_words,
            "first_group_pass": first_group_pass,
            "turn_group": turn_group,
            "store_group": store_group,
            "add_values": add_values,
        }

        def run(entries):
            for entry in entries:
                calls[entry[0]](*entry[1:])

        run(HEAD)
        last_unit = UNITS - 1
        for i in range(UNITS):
            if i >= J:
                for k_pass in range(3):
                    one_pass(i, k_pass)
            run(TENSOR_STEP.get(i, []))
            if i < last_unit:
                square(i)
            if i >= 1:
                reciprocal_root(i - 1)
            run(SCALAR_STEP.get(i, []))
            if i >= 1:
                weigh(i - 1)
            run(VECTOR_STEP.get(i, []))
            run(GPSIMD_STEP.get(i, []))

        halves = ((0, W // 2), (W // 2, W))
        for start, stop in halves:
            square(last_unit, start, stop)
            reciprocal_root(last_unit, start, stop)
        slices = []
        for s in range(4):
            if s < 8 - Z_BANKS:
                slices.append(turn_banks.tile([P, P], F32, name="turned"))
            else:
                slices.append(z_banks.tile([P, P], F32, name="z"))
        rest = left[GROUPS - 1]
        for i in rest[:-1]:
            for s in range(4):
                turn_and_add(slices[s][:], i, s, i == rest[0], False)
        for start, stop in halves:
            weigh(last_unit, start, stop)
        for s in range(4):
            turn_and_add(slices[s][:], last_unit, s, False, True)
        result = stage.tile([P, 4, P], F32, name="result")
        for s in range(0, 4, 2):
            nc.vector.tensor_copy(out=result[:, s, :], in_=slices[s][:])
            nc.scalar.copy(out=result[:, s + 1, :], in_=slices[s + 1][:])
            nc.sync.dma_start(out=out_view[3, 1][:, s : s + 2, :], in_=result[:, s : s + 2, :])
